import numpy as np
import ml_dtypes


def mxq(x, axis, fmt="e4m3"):
    dtype, down = {"e4m3": (ml_dtypes.float8_e4m3fn, 7), "e5m2": (ml_dtypes.float8_e5m2, 14)}[fmt]
    v = np.moveaxis(np.asarray(x, np.float32).astype(ml_dtypes.bfloat16).astype(np.float64), axis, -1)
    blocks = v.reshape(v.shape[:-1] + (-1, 32))
    amax = np.abs(blocks).max(-1, keepdims=True)
    byte = np.maximum(np.where(amax > 0, np.frexp(amax)[1] - 1 + 127, 0) - down, 1)
    scale = np.exp2(byte - 127.0)
    codes = (blocks / scale).astype(np.float32).astype(dtype).astype(np.float64)
    return np.moveaxis((codes * scale).reshape(v.shape), -1, axis)


WIDE = False


def mx_kscale(k):
    if not WIDE:
        return np.ones(k)
    levels = np.array([10, -10, 5, -5, 0])
    if k % 512:
        return np.exp2(np.random.permutation(np.resize(levels, k // 32))).repeat(32)
    a = np.empty((k // 512, 16))
    for p in range(k // 512):
        a[p, :8] = np.random.permutation(np.resize(levels, 8))
        for g in range(8):
            far = levels[np.abs(levels - a[p, g]) >= 10]
            a[p, g + 8] = far[np.random.randint(len(far))]
    return np.exp2(a.ravel()).repeat(32)


def f64(x):
    return np.asarray(x).astype(np.float64)


def striped(idx):
    return np.tile(np.asarray(idx).reshape(-1, 16).T, (8, 1)).astype(np.uint16)


def unstriped(offs):
    return offs[:16].T.reshape(-1).astype(np.int64)


E2M1 = np.array([0.0, 0.5, 1.0, 1.5, 2.0, 3.0, 4.0, 6.0, -0.0, -0.5, -1.0, -1.5, -2.0, -3.0, -4.0, -6.0])


def pack_weight(w, fmt):
    k, n = w.shape
    w = f64(np.asarray(w, np.float32).astype(ml_dtypes.bfloat16)).reshape(k // 32, 32, n)
    amax = np.abs(w).max(1)
    if fmt == "e4m3":
        byte = np.frexp(amax)[1] - 1 + 127 - 7
    else:
        mant, ex = np.frexp(amax / 6.0)
        byte = np.where(mant > 0.5, ex, ex - 1) + 127
    byte = np.clip(np.where(amax > 0, byte, 1), 1, 254)
    scaled = (w * np.exp2(127.0 - byte)[:, None, :]).reshape(k, n).astype(np.float32)
    by_word = np.ascontiguousarray(scaled.reshape(k // 512, 128, 4, n).transpose(0, 1, 3, 2))
    if fmt == "e4m3":
        words = by_word.astype(ml_dtypes.float8_e4m3fn).view(np.uint8)
    else:
        c = by_word.astype(ml_dtypes.float4_e2m1fn).view(np.uint8) & 0xF
        words = (c[..., 0::2] | (c[..., 1::2] << 4)).reshape(k // 512, 128, 2 * n)
    return np.ascontiguousarray(words), np.ascontiguousarray(byte.astype(np.uint8).reshape(k // 512, 16, n))


def unpack_weight(words, scales, fmt):
    g, _, n = scales.shape
    words = np.ascontiguousarray(words).reshape(g, 128, n, -1)
    if fmt == "e4m3":
        vals = words.view(ml_dtypes.float8_e4m3fn).astype(np.float64)
    else:
        nib = np.empty((g, 128, n, 4), np.uint8)
        nib[..., 0::2] = words & 0xF
        nib[..., 1::2] = words >> 4
        vals = E2M1[nib]
    vals = vals * np.repeat(np.exp2(scales.astype(np.float64) - 127.0), 8, axis=1)[..., None]
    return vals.transpose(0, 1, 3, 2).reshape(g * 512, n)


D, E, T, I, Q = 512, 512, 2048, 512, 128


def setup_inputs():
    n = np.random.standard_normal
    idx = np.random.permutation(T)[:I]
    fd = mx_kscale(D)
    fe = mx_kscale(E)
    keysp = pack_weight(n((D, T)) / fd[:, None], "e4m3")
    valsp = pack_weight(n((E, T)) / fe[:, None], "e4m3")
    return {
        "query": (n((D, Q)) * 1.0 / np.sqrt(D) * fd[:, None]).astype(np.float32),
        "keys_words": keysp[0],
        "keys_scales": keysp[1],
        "aim": (np.random.uniform(0.5, 2.0, (Q, 1))).astype(np.float32),
        "soft": (np.random.uniform(0.5, 2.0, (Q, 1))).astype(np.float32),
        "gout": (n((E, Q)) * 1 / np.sqrt(E) * fe[:, None]).astype(np.float32),
        "vals_words": valsp[0],
        "vals_scales": valsp[1],
        "dquery": (n((D, Q)) * 1.0 / np.sqrt(D) * fd[:, None]).astype(np.float32),
        "base": (0.5 * n((Q, T))).astype(np.float32),
        "offs": striped(idx),
    }


def reference(query, keys_words, keys_scales, aim, soft, gout, vals_words, vals_scales, dquery, base, offs):
    idx = unstriped(offs)
    keysu = unpack_weight(keys_words, keys_scales, "e4m3")
    valsu = unpack_weight(vals_words, vals_scales, "e4m3")
    queryq = mxq(f64(query), 0, "e4m3")
    keysidxg = keysu[:, idx]
    a = queryq.T @ keysidxg
    dqueryq = mxq(f64(dquery), 0, "e4m3")
    ta = dqueryq.T @ keysidxg
    p = 1.0 / (np.square(f64(aim) - a) + f64(soft))
    z = np.sum(p, axis=1, keepdims=True)
    goutq = mxq(f64(gout), 0, "e4m3")
    valsidxg = valsu[:, idx]
    c0 = goutq.T @ valsidxg
    dz = np.sum(c0 * p / np.square(z) * (-1.0), axis=1, keepdims=True)
    dp = c0 / z + dz
    tp = ta * (-1.0) * (f64(aim) - a) * 2.0 * (-1.0) / np.square(np.square(f64(aim) - a) + f64(soft))
    tz = np.sum(tp, axis=1, keepdims=True)
    tdz = np.sum((tp * c0 - tz * z * 2.0 * c0 * p / np.square(z)) / np.square(z) * (-1.0), axis=1, keepdims=True)
    tdp = tz * c0 / np.square(z) * (-1.0) + tdz
    tda = ((tdp * (-1.0) - ta * (-1.0) * (f64(aim) - a) * 2.0 * (np.square(f64(aim) - a) + f64(soft)) * 2.0 * dp * (-1.0) / np.square(np.square(f64(aim) - a) + f64(soft))) / np.square(np.square(f64(aim) - a) + f64(soft)) * (f64(aim) - a) + ta * (-1.0) * dp * (-1.0) / np.square(np.square(f64(aim) - a) + f64(soft))) * 2.0 * (-1.0)
    gs = tda * 512.0
    gf = np.zeros((Q, T))
    gf[:, idx] = gs
    y = f64(base) + gf
    return y

@@ -1,0 +1,174 @@
+from contextlib import ExitStack
+
+import concourse.mybir as mybir
+
+D, E, T, I, Q = 512, 512, 2048, 512, 128
+FLOPS = 3 * 2 * 512 * Q * I
+
+F32 = mybir.dt.float32
+BF16 = mybir.dt.bfloat16
+I32 = mybir.dt.int32
+U32 = mybir.dt.uint32
+U16 = mybir.dt.uint16
+U8 = mybir.dt.uint8
+FP8X4 = mybir.dt.float8_e4m3fn_x4
+ALU = mybir.AluOpType
+ACT = mybir.ActivationFunctionType
+
+P = 128
+PACK = 4
+HALF = I // 2
+KEY_ROW = 0
+VAL_ROW = 4
+STORE = [512, 512, 512, 512]
+
+
+def tile_attend_hvnearpoint_s_kernel(tc, query, keys_words, keys_scales, aim, soft, gout, vals_words, vals_scales, dquery, base, offs, out):
+    nc = tc.nc
+    with ExitStack() as ctx:
+        sb = ctx.enter_context(tc.tile_pool(name="sb", bufs=1))
+        ps = ctx.enter_context(tc.psum_pool(name="ps", bufs=1))
+
+        def tile(name, shape, dtype, tag=None):
+            return sb.tile(shape, dtype, name=name, tag=tag or name, align_bytes=64)
+
+        offsets = sb.tile([P, I // 16], U16, name="offsets")
+        key_pool = tile("key_pool", [P, T], I32)
+        val_pool = tile("val_pool", [P, T], I32)
+        key_scale_pool = tile("key_scale_pool", [P, T], U8)
+        val_scale_pool = tile("val_scale_pool", [P, T], U8)
+        query_raw = tile("query_raw", [P, PACK, Q], F32)
+        dquery_raw = tile("dquery_raw", [P, PACK, Q], F32)
+        gout_raw = tile("gout_raw", [P, PACK, Q], F32)
+        base_sb = tile("base_sb", [P, T], F32)
+        aim_col = tile("aim_col", [P, 1], F32)
+        soft_col = tile("soft_col", [P, 1], F32)
+        placed = tile("placed", [P, T], F32)
+
+        nc.gpsimd.memset(key_scale_pool[:].bitcast(I32), 0)
+        nc.vector.memset(val_scale_pool[:].bitcast(I32), 0)
+        nc.vector.memset(placed[:], 0.0)
+
+        def load_rows(dst, src):
+            nc.sync.dma_start(out=dst[:], in_=src.rearrange("(p j) w -> p j w", j=PACK))
+
+        def load_words(dst, src):
+            nc.sync.dma_start(out=dst[:], in_=src[0].rearrange("p n t -> p (n t)").bitcast(I32))
+
+        def load_scales(dst, src, first):
+            for quad in range(4):
+                rows = slice(32 * quad + first, 32 * quad + first + 4)
+                nc.sync.dma_start(out=dst[rows, :].bitcast(I32), in_=src[0, 4 * quad : 4 * quad + 4, :].bitcast(I32))
+
+        nc.sync.dma_start(offsets[:], offs)
+        load_rows(query_raw, query)
+        load_rows(dquery_raw, dquery)
+        load_rows(gout_raw, gout)
+        load_scales(key_scale_pool, keys_scales, KEY_ROW)
+        load_words(key_pool, keys_words)
+        load_scales(val_scale_pool, vals_scales, VAL_ROW)
+        nc.sync.dma_start(out=aim_col[:], in_=aim)
+        nc.sync.dma_start(out=soft_col[:], in_=soft)
+        load_words(val_pool, vals_words)
+        nc.sync.dma_start(out=base_sb[:], in_=base)
+
+        def interleave(dst, raw):
+            nc.scalar.copy(
+                out=dst.rearrange("p (c i) t -> p c t i", i=4),
+                in_=raw[:].rearrange("p t (c i) -> p c t i", i=4),
+            )
+
+        def quantise(codes, scales, grouped):
+            nc.vector.quantize_mx(out=codes[:].bitcast(FP8X4), scales=scales[:], in_=grouped[:].rearrange("p w j -> p (w j)"))
+
+        key_scales = tile("key_scales", [P, I], U8)
+        nc.vector.tensor_copy(key_scales[:], key_scale_pool[:].indirect(offsets[:]))
+
+        qd_grouped = tile("qd_grouped", [P, 2 * Q, PACK], BF16)
+        qd_codes = tile("qd_codes", [P, 2 * Q], U32)
+        qd_scales = tile("qd_scales", [P, 2 * Q], U8)
+        interleave(qd_grouped[:, :Q, :], query_raw)
+        interleave(qd_grouped[:, Q:, :], dquery_raw)
+        quantise(qd_codes, qd_scales, qd_grouped)
+        g_grouped = tile("g_grouped", [P, Q, PACK], BF16)
+        g_codes = tile("g_codes", [P, Q], U32)
+        g_scales = tile("g_scales", [P, Q], U8)
+        interleave(g_grouped[:], gout_raw)
+        quantise(g_codes, g_scales, g_grouped)
+
+        key_words = tile("key_words", [P, I], U32)
+        halves = [slice(0, HALF), slice(HALF, I)]
+        score = [ps.tile([P, HALF], F32, name="score%d" % h) for h in range(2)]
+        dscore = ps.tile([P, I], F32, name="dscore")
+        c0 = ps.tile([P, I], F32, name="c0")
+        for h, cols in enumerate(halves):
+            nc.vector.tensor_copy(key_words[:, cols], key_pool[:].bitcast(U32).indirect(offsets[:, 16 * h : 16 * h + 16]))
+            nc.tensor.matmul_mx(
+                out=score[h][:], lhsT=qd_codes[:, :Q].bitcast(FP8X4), lhsT_scale=qd_scales[:, :Q],
+                rhs=key_words[:, cols].bitcast(FP8X4), rhs_scale=key_scales[KEY_ROW:, cols], start=True, stop=True,
+            )
+        nc.tensor.matmul_mx(
+            out=dscore[:], lhsT=qd_codes[:, Q:].bitcast(FP8X4), lhsT_scale=qd_scales[:, Q:],
+            rhs=key_words[:].bitcast(FP8X4), rhs_scale=key_scales[KEY_ROW:, :], start=True, stop=True,
+        )
+
+        gap = tile("gap", [P, I], F32)
+        gap_sq = tile("gap_sq", [P, I], F32)
+        root = tile("root", [P, I], F32)
+        part = tile("part", [P, I], F32)
+        part_sq = tile("part_sq", [P, I], F32)
+        bend = tile("bend", [P, I], F32)
+        z = tile("z", [P, 1], F32)
+        for h, cols in enumerate(halves):
+            nc.scalar.activation(gap_sq[:, cols], score[h][:], ACT.Square, bias=aim_col[:], scale=-1.0)
+            nc.scalar.activation(gap[:, cols], score[h][:], ACT.Identity, bias=aim_col[:], scale=-1.0)
+            nc.scalar.activation(root[:, cols], gap_sq[:, cols], ACT.Abs_reciprocal_sqrt, bias=soft_col[:], scale=1.0)
+        nc.scalar.activation(part[:], root[:], ACT.Square, accum_out=z[:])
+        nc.scalar.activation(part_sq[:], part[:], ACT.Square, scale=32.0)
+        nc.scalar.activation(bend[:], part[:], ACT.Identity, bias=-0.75, scale=soft_col[:])
+
+        val_scales = tile("val_scales", [P, I], U8)
+        nc.vector.tensor_copy(val_scales[:], val_scale_pool[:].indirect(offsets[:]))
+        val_words = tile("val_words", [P, I], U32)
+        nc.vector.tensor_copy(val_words[:], val_pool[:].bitcast(U32).indirect(offsets[:]))
+        nc.tensor.matmul_mx(
+            out=c0[:], lhsT=g_codes[:].bitcast(FP8X4), lhsT_scale=g_scales[:],
+            rhs=val_words[:].bitcast(FP8X4), rhs_scale=val_scales[VAL_ROW:, :], start=True, stop=True,
+        )
+
+        late = tile("late", [P, 2 * I + 16], F32, tag="val_pool")
+        tw = late[:, :I]
+        tu = late[:, I : 2 * I]
+        rz = late[:, 2 * I : 2 * I + 1]
+        rho = tile("rho", [P, 1], F32)
+        mean = tile("mean", [P, 1], F32)
+        bsum = tile("bsum", [P, 1], F32)
+        negb = tile("negb", [P, 1], F32)
+        tpz = tile("tpz", [P, I], F32)
+        prod_m = tile("prod_m", [P, I], F32)
+        prod_b = tile("prod_b", [P, I], F32)
+        negk = tile("negk", [P, I], F32)
+        negx = tile("negx", [P, I], F32)
+        y = tile("y", [P, I], F32)
+        nc.vector.scalar_tensor_tensor(tu, dscore[:], 2.0 / 1024.0, gap[:], ALU.mult, ALU.mult)
+        nc.vector.reciprocal(rz, z[:])
+        nc.vector.scalar_tensor_tensor(prod_m[:], c0[:], rz, part[:], ALU.mult, ALU.mult, accum_out=mean[:])
+        nc.vector.scalar_tensor_tensor(tpz[:], tu, rz, part_sq[:], ALU.mult, ALU.mult, accum_out=rho[:])
+        nc.vector.scalar_tensor_tensor(tw, dscore[:], -4.0, bend[:], ALU.mult, ALU.mult)
+        nc.vector.scalar_tensor_tensor(prod_b[:], c0[:], 1.0, tpz[:], ALU.mult, ALU.mult, accum_out=bsum[:])
+        for cols in halves:
+            nc.vector.scalar_tensor_tensor(negk[:, cols], gap[:, cols], rho[:], tw[:, cols], ALU.mult, ALU.subtract)
+        nc.vector.tensor_scalar(negb[:], mean[:], rho[:], bsum[:], ALU.mult, ALU.subtract)
+        for cols in halves:
+            nc.vector.scalar_tensor_tensor(negx[:, cols], c0[:, cols], mean[:], negk[:, cols], ALU.subtract, ALU.mult)
+        for cols in halves:
+            nc.vector.scalar_tensor_tensor(y[:, cols], gap[:, cols], negb[:], negx[:, cols], ALU.mult, ALU.subtract)
+        nc.vector.tensor_tensor(placed[:].indirect(offsets[:]), y[:], part_sq[:], ALU.mult)
+
+        first = 0
+        for n, width in enumerate(STORE):
+            cols = slice(first, first + width)
+            result = tile("result%d" % n, [P, width], F32)
+            nc.vector.scalar_tensor_tensor(result[:], placed[:, cols], rz, base_sb[:, cols], ALU.mult, ALU.add)
+            nc.sync.dma_start(out=out[:, cols], in_=result[:])
+            first = first + width

@@ -46,6 +46,10 @@ def tile_attend_hvnearpoint_s_kernel(tc, query, keys_words, keys_scales, aim, so
         placed = tile("placed", [P, T], F32)
 
         nc.gpsimd.memset(key_scale_pool[:].bitcast(I32), 0)
+        warm_in = tile("warm_in", [P, 1], F32)
+        warm_out = tile("warm_out", [P, 1], F32)
+        nc.vector.memset(warm_in[:], 1.0)
+        nc.scalar.activation(warm_out[:], warm_in[:], ACT.Abs_reciprocal_sqrt)
         nc.vector.memset(val_scale_pool[:].bitcast(I32), 0)
         nc.vector.memset(placed[:], 0.0)
 

@@ -60,24 +60,23 @@ def tile_attend_hvnearpoint_s_kernel(tc, query, keys_words, keys_scales, aim, so
             nc.sync.dma_start(out=dst[:], in_=src[0].rearrange("p n t -> p (n t)").bitcast(I32))
 
         def load_scales(dst, src, first):
-            for quad in range(4):
-                rows = slice(32 * quad + first, 32 * quad + first + 4)
-                nc.sync.dma_start(out=dst[rows, :].bitcast(I32), in_=src[0, 4 * quad : 4 * quad + 4, :].bitcast(I32))
+            for r in range(4):
+                nc.sync.dma_start(out=dst[first + r : P : 32, :].bitcast(I32), in_=src[0, r:16:4, :].bitcast(I32))
 
         nc.sync.dma_start(offsets[:], offs)
         load_rows(query_raw, query)
         load_rows(dquery_raw, dquery)
-        load_rows(gout_raw, gout)
         load_scales(key_scale_pool, keys_scales, KEY_ROW)
         load_words(key_pool, keys_words)
-        load_scales(val_scale_pool, vals_scales, VAL_ROW)
+        nc.gpsimd.dma_start(out=soft_col[:], in_=soft)
         nc.sync.dma_start(out=aim_col[:], in_=aim)
-        nc.sync.dma_start(out=soft_col[:], in_=soft)
+        load_rows(gout_raw, gout)
+        load_scales(val_scale_pool, vals_scales, VAL_ROW)
         load_words(val_pool, vals_words)
         nc.sync.dma_start(out=base_sb[:], in_=base)
 
-        def interleave(dst, raw):
-            nc.scalar.copy(
+        def interleave(copy, dst, raw):
+            copy(
                 out=dst.rearrange("p (c i) t -> p c t i", i=4),
                 in_=raw[:].rearrange("p t (c i) -> p c t i", i=4),
             )
@@ -88,17 +87,16 @@ def tile_attend_hvnearpoint_s_kernel(tc, query, keys_words, keys_scales, aim, so
         key_scales = tile("key_scales", [P, I], U8)
         nc.vector.tensor_copy(key_scales[:], key_scale_pool[:].indirect(offsets[:]))
 
-        qd_grouped = tile("qd_grouped", [P, 2 * Q, PACK], BF16)
-        qd_codes = tile("qd_codes", [P, 2 * Q], U32)
-        qd_scales = tile("qd_scales", [P, 2 * Q], U8)
-        interleave(qd_grouped[:, :Q, :], query_raw)
-        interleave(qd_grouped[:, Q:, :], dquery_raw)
-        quantise(qd_codes, qd_scales, qd_grouped)
-        g_grouped = tile("g_grouped", [P, Q, PACK], BF16)
-        g_codes = tile("g_codes", [P, Q], U32)
-        g_scales = tile("g_scales", [P, Q], U8)
-        interleave(g_grouped[:], gout_raw)
-        quantise(g_codes, g_scales, g_grouped)
+        def stationary(name, raw, copy):
+            grouped = tile(name + "_grouped", [P, Q, PACK], BF16)
+            codes = tile(name + "_codes", [P, Q], U32)
+            scales = tile(name + "_scales", [P, Q], U8)
+            interleave(copy, grouped[:], raw)
+            quantise(codes, scales, grouped)
+            return codes, scales
+
+        q_codes, q_scales = stationary("query", query_raw, nc.vector.tensor_copy)
+        dq_codes, dq_scales = stationary("dquery", dquery_raw, nc.scalar.copy)
 
         key_words = tile("key_words", [P, I], U32)
         halves = [slice(0, HALF), slice(HALF, I)]
@@ -108,24 +106,27 @@ def tile_attend_hvnearpoint_s_kernel(tc, query, keys_words, keys_scales, aim, so
         for h, cols in enumerate(halves):
             nc.vector.tensor_copy(key_words[:, cols], key_pool[:].bitcast(U32).indirect(offsets[:, 16 * h : 16 * h + 16]))
             nc.tensor.matmul_mx(
-                out=score[h][:], lhsT=qd_codes[:, :Q].bitcast(FP8X4), lhsT_scale=qd_scales[:, :Q],
+                out=score[h][:], lhsT=q_codes[:].bitcast(FP8X4), lhsT_scale=q_scales[:],
                 rhs=key_words[:, cols].bitcast(FP8X4), rhs_scale=key_scales[KEY_ROW:, cols], start=True, stop=True,
             )
         nc.tensor.matmul_mx(
-            out=dscore[:], lhsT=qd_codes[:, Q:].bitcast(FP8X4), lhsT_scale=qd_scales[:, Q:],
+            out=dscore[:], lhsT=dq_codes[:].bitcast(FP8X4), lhsT_scale=dq_scales[:],
             rhs=key_words[:].bitcast(FP8X4), rhs_scale=key_scales[KEY_ROW:, :], start=True, stop=True,
         )
 
-        gap = tile("gap", [P, I], F32)
-        gap_sq = tile("gap_sq", [P, I], F32)
+        g_codes, g_scales = stationary("gout", gout_raw, nc.scalar.copy)
+        gaps = tile("gaps", [P, 2 * I], F32, tag="gout_raw")
+        gap = gaps[:, :I]
+        gap_sq = gaps[:, I:]
         root = tile("root", [P, I], F32)
         part = tile("part", [P, I], F32)
         part_sq = tile("part_sq", [P, I], F32)
         bend = tile("bend", [P, I], F32)
         z = tile("z", [P, 1], F32)
         for h, cols in enumerate(halves):
-            nc.scalar.activation(gap_sq[:, cols], score[h][:], ACT.Square, bias=aim_col[:], scale=-1.0)
             nc.scalar.activation(gap[:, cols], score[h][:], ACT.Identity, bias=aim_col[:], scale=-1.0)
+            nc.scalar.activation(gap_sq[:, cols], score[h][:], ACT.Square, bias=aim_col[:], scale=-1.0)
+        for cols in halves:
             nc.scalar.activation(root[:, cols], gap_sq[:, cols], ACT.Abs_reciprocal_sqrt, bias=soft_col[:], scale=1.0)
         nc.scalar.activation(part[:], root[:], ACT.Square, accum_out=z[:])
         nc.scalar.activation(part_sq[:], part[:], ACT.Square, scale=32.0)
@@ -133,6 +134,8 @@ def tile_attend_hvnearpoint_s_kernel(tc, query, keys_words, keys_scales, aim, so
 
         val_scales = tile("val_scales", [P, I], U8)
         nc.vector.tensor_copy(val_scales[:], val_scale_pool[:].indirect(offsets[:]))
+        tu = tile("tu", [P, I], F32, tag="val_scale_pool")
+        nc.vector.scalar_tensor_tensor(tu[:], dscore[:], 2.0 / 1024.0, gap, ALU.mult, ALU.mult)
         val_words = tile("val_words", [P, I], U32)
         nc.vector.tensor_copy(val_words[:], val_pool[:].bitcast(U32).indirect(offsets[:]))
         nc.tensor.matmul_mx(
@@ -140,10 +143,9 @@ def tile_attend_hvnearpoint_s_kernel(tc, query, keys_words, keys_scales, aim, so
             rhs=val_words[:].bitcast(FP8X4), rhs_scale=val_scales[VAL_ROW:, :], start=True, stop=True,
         )
 
-        late = tile("late", [P, 2 * I + 16], F32, tag="val_pool")
+        late = tile("late", [P, I + 16], F32, tag="val_pool")
         tw = late[:, :I]
-        tu = late[:, I : 2 * I]
-        rz = late[:, 2 * I : 2 * I + 1]
+        rz = late[:, I : I + 1]
         rho = tile("rho", [P, 1], F32)
         mean = tile("mean", [P, 1], F32)
         bsum = tile("bsum", [P, 1], F32)
@@ -154,17 +156,15 @@ def tile_attend_hvnearpoint_s_kernel(tc, query, keys_words, keys_scales, aim, so
         negk = tile("negk", [P, I], F32)
         negx = tile("negx", [P, I], F32)
         y = tile("y", [P, I], F32)
-        nc.vector.scalar_tensor_tensor(tu, dscore[:], 2.0 / 1024.0, gap[:], ALU.mult, ALU.mult)
         nc.vector.reciprocal(rz, z[:])
-        nc.vector.scalar_tensor_tensor(prod_m[:], c0[:], rz, part[:], ALU.mult, ALU.mult, accum_out=mean[:])
-        nc.vector.scalar_tensor_tensor(tpz[:], tu, rz, part_sq[:], ALU.mult, ALU.mult, accum_out=rho[:])
+        nc.vector.scalar_tensor_tensor(tpz[:], tu[:], rz, part_sq[:], ALU.mult, ALU.mult, accum_out=rho[:])
         nc.vector.scalar_tensor_tensor(tw, dscore[:], -4.0, bend[:], ALU.mult, ALU.mult)
+        nc.vector.scalar_tensor_tensor(prod_m[:], c0[:], rz, part[:], ALU.mult, ALU.mult, accum_out=mean[:])
+        nc.vector.scalar_tensor_tensor(negk[:], gap, rho[:], tw, ALU.mult, ALU.subtract)
         nc.vector.scalar_tensor_tensor(prod_b[:], c0[:], 1.0, tpz[:], ALU.mult, ALU.mult, accum_out=bsum[:])
-        for cols in halves:
-            nc.vector.scalar_tensor_tensor(negk[:, cols], gap[:, cols], rho[:], tw[:, cols], ALU.mult, ALU.subtract)
+        nc.vector.scalar_tensor_tensor(negx[:, halves[0]], c0[:, halves[0]], mean[:], negk[:, halves[0]], ALU.subtract, ALU.mult)
         nc.vector.tensor_scalar(negb[:], mean[:], rho[:], bsum[:], ALU.mult, ALU.subtract)
-        for cols in halves:
-            nc.vector.scalar_tensor_tensor(negx[:, cols], c0[:, cols], mean[:], negk[:, cols], ALU.subtract, ALU.mult)
+        nc.vector.scalar_tensor_tensor(negx[:, halves[1]], c0[:, halves[1]], mean[:], negk[:, halves[1]], ALU.subtract, ALU.mult)
         for cols in halves:
             nc.vector.scalar_tensor_tensor(y[:, cols], gap[:, cols], negb[:], negx[:, cols], ALU.mult, ALU.subtract)
         nc.vector.tensor_tensor(placed[:].indirect(offsets[:]), y[:], part_sq[:], ALU.mult)

from contextlib import ExitStack

import concourse.mybir as mybir

D, E, T, I, Q = 512, 512, 2048, 512, 128
FLOPS = 3 * 2 * 512 * Q * I

F32 = mybir.dt.float32
BF16 = mybir.dt.bfloat16
I32 = mybir.dt.int32
U32 = mybir.dt.uint32
U16 = mybir.dt.uint16
U8 = mybir.dt.uint8
FP8X4 = mybir.dt.float8_e4m3fn_x4
ALU = mybir.AluOpType
ACT = mybir.ActivationFunctionType

P = 128
PACK = 4
HALF = I // 2
KEY_ROW = 0
VAL_ROW = 4
STORE = [512, 512, 512, 512]


def tile_attend_hvnearpoint_s_kernel(tc, query, keys_words, keys_scales, aim, soft, gout, vals_words, vals_scales, dquery, base, offs, out):
    nc = tc.nc
    with ExitStack() as ctx:
        sb = ctx.enter_context(tc.tile_pool(name="sb", bufs=1))
        ps = ctx.enter_context(tc.psum_pool(name="ps", bufs=1))

        def tile(name, shape, dtype, tag=None):
            return sb.tile(shape, dtype, name=name, tag=tag or name, align_bytes=64)

        offsets = sb.tile([P, I // 16], U16, name="offsets")
        key_pool = tile("key_pool", [P, T], I32)
        val_pool = tile("val_pool", [P, T], I32)
        key_scale_pool = tile("key_scale_pool", [P, T], U8)
        val_scale_pool = tile("val_scale_pool", [P, T], U8)
        query_raw = tile("query_raw", [P, PACK, Q], F32)
        dquery_raw = tile("dquery_raw", [P, PACK, Q], F32)
        gout_raw = tile("gout_raw", [P, PACK, Q], F32)
        base_sb = tile("base_sb", [P, T], F32)
        aim_col = tile("aim_col", [P, 1], F32)
        soft_col = tile("soft_col", [P, 1], F32)
        placed = tile("placed", [P, T], F32)

        nc.gpsimd.memset(key_scale_pool[:].bitcast(I32), 0)
        warm_in = tile("warm_in", [P, 1], F32)
        warm_out = tile("warm_out", [P, 1], F32)
        nc.vector.memset(warm_in[:], 1.0)
        nc.scalar.activation(warm_out[:], warm_in[:], ACT.Abs_reciprocal_sqrt)
        nc.vector.memset(val_scale_pool[:].bitcast(I32), 0)
        nc.vector.memset(placed[:], 0.0)

        def load_rows(dst, src):
            nc.sync.dma_start(out=dst[:], in_=src.rearrange("(p j) w -> p j w", j=PACK))

        def load_words(dst, src):
            nc.sync.dma_start(out=dst[:], in_=src[0].rearrange("p n t -> p (n t)").bitcast(I32))

        def load_scales(dst, src, first):
            for r in range(4):
                nc.sync.dma_start(out=dst[first + r : P : 32, :].bitcast(I32), in_=src[0, r:16:4, :].bitcast(I32))

        nc.sync.dma_start(offsets[:], offs)
        load_rows(query_raw, query)
        load_rows(dquery_raw, dquery)
        load_scales(key_scale_pool, keys_scales, KEY_ROW)
        load_words(key_pool, keys_words)
        nc.gpsimd.dma_start(out=soft_col[:], in_=soft)
        nc.sync.dma_start(out=aim_col[:], in_=aim)
        load_rows(gout_raw, gout)
        load_scales(val_scale_pool, vals_scales, VAL_ROW)
        load_words(val_pool, vals_words)
        nc.sync.dma_start(out=base_sb[:], in_=base)

        def interleave(copy, dst, raw):
            copy(
                out=dst.rearrange("p (c i) t -> p c t i", i=4),
                in_=raw[:].rearrange("p t (c i) -> p c t i", i=4),
            )

        def quantise(codes, scales, grouped):
            nc.vector.quantize_mx(out=codes[:].bitcast(FP8X4), scales=scales[:], in_=grouped[:].rearrange("p w j -> p (w j)"))

        key_scales = tile("key_scales", [P, I], U8)
        nc.vector.tensor_copy(key_scales[:], key_scale_pool[:].indirect(offsets[:]))

        def stationary(name, raw, copy):
            grouped = tile(name + "_grouped", [P, Q, PACK], BF16)
            codes = tile(name + "_codes", [P, Q], U32)
            scales = tile(name + "_scales", [P, Q], U8)
            interleave(copy, grouped[:], raw)
            quantise(codes, scales, grouped)
            return codes, scales

        q_codes, q_scales = stationary("query", query_raw, nc.vector.tensor_copy)
        dq_codes, dq_scales = stationary("dquery", dquery_raw, nc.scalar.copy)

        key_words = tile("key_words", [P, I], U32)
        halves = [slice(0, HALF), slice(HALF, I)]
        score = [ps.tile([P, HALF], F32, name="score%d" % h) for h in range(2)]
        dscore = ps.tile([P, I], F32, name="dscore")
        c0 = ps.tile([P, I], F32, name="c0")
        for h, cols in enumerate(halves):
            nc.vector.tensor_copy(key_words[:, cols], key_pool[:].bitcast(U32).indirect(offsets[:, 16 * h : 16 * h + 16]))
            nc.tensor.matmul_mx(
                out=score[h][:], lhsT=q_codes[:].bitcast(FP8X4), lhsT_scale=q_scales[:],
                rhs=key_words[:, cols].bitcast(FP8X4), rhs_scale=key_scales[KEY_ROW:, cols], start=True, stop=True,
            )
        nc.tensor.matmul_mx(
            out=dscore[:], lhsT=dq_codes[:].bitcast(FP8X4), lhsT_scale=dq_scales[:],
            rhs=key_words[:].bitcast(FP8X4), rhs_scale=key_scales[KEY_ROW:, :], start=True, stop=True,
        )

        g_codes, g_scales = stationary("gout", gout_raw, nc.scalar.copy)
        gaps = tile("gaps", [P, 2 * I], F32, tag="gout_raw")
        gap = gaps[:, :I]
        gap_sq = gaps[:, I:]
        root = tile("root", [P, I], F32)
        part = tile("part", [P, I], F32)
        part_sq = tile("part_sq", [P, I], F32)
        bend = tile("bend", [P, I], F32)
        z = tile("z", [P, 1], F32)
        for h, cols in enumerate(halves):
            nc.scalar.activation(gap[:, cols], score[h][:], ACT.Identity, bias=aim_col[:], scale=-1.0)
            nc.scalar.activation(gap_sq[:, cols], score[h][:], ACT.Square, bias=aim_col[:], scale=-1.0)
        for cols in halves:
            nc.scalar.activation(root[:, cols], gap_sq[:, cols], ACT.Abs_reciprocal_sqrt, bias=soft_col[:], scale=1.0)
        nc.scalar.activation(part[:], root[:], ACT.Square, accum_out=z[:])
        nc.scalar.activation(part_sq[:], part[:], ACT.Square, scale=32.0)
        nc.scalar.activation(bend[:], part[:], ACT.Identity, bias=-0.75, scale=soft_col[:])

        val_scales = tile("val_scales", [P, I], U8)
        nc.vector.tensor_copy(val_scales[:], val_scale_pool[:].indirect(offsets[:]))
        tu = tile("tu", [P, I], F32, tag="val_scale_pool")
        nc.vector.scalar_tensor_tensor(tu[:], dscore[:], 2.0 / 1024.0, gap, ALU.mult, ALU.mult)
        val_words = tile("val_words", [P, I], U32)
        nc.vector.tensor_copy(val_words[:], val_pool[:].bitcast(U32).indirect(offsets[:]))
        nc.tensor.matmul_mx(
            out=c0[:], lhsT=g_codes[:].bitcast(FP8X4), lhsT_scale=g_scales[:],
            rhs=val_words[:].bitcast(FP8X4), rhs_scale=val_scales[VAL_ROW:, :], start=True, stop=True,
        )

        late = tile("late", [P, I + 16], F32, tag="val_pool")
        tw = late[:, :I]
        rz = late[:, I : I + 1]
        rho = tile("rho", [P, 1], F32)
        mean = tile("mean", [P, 1], F32)
        bsum = tile("bsum", [P, 1], F32)
        negb = tile("negb", [P, 1], F32)
        tpz = tile("tpz", [P, I], F32)
        prod_m = tile("prod_m", [P, I], F32)
        prod_b = tile("prod_b", [P, I], F32)
        negk = tile("negk", [P, I], F32)
        negx = tile("negx", [P, I], F32)
        y = tile("y", [P, I], F32)
        nc.vector.reciprocal(rz, z[:])
        nc.vector.scalar_tensor_tensor(tpz[:], tu[:], rz, part_sq[:], ALU.mult, ALU.mult, accum_out=rho[:])
        nc.vector.scalar_tensor_tensor(tw, dscore[:], -4.0, bend[:], ALU.mult, ALU.mult)
        nc.vector.scalar_tensor_tensor(prod_m[:], c0[:], rz, part[:], ALU.mult, ALU.mult, accum_out=mean[:])
        nc.vector.scalar_tensor_tensor(negk[:], gap, rho[:], tw, ALU.mult, ALU.subtract)
        nc.vector.scalar_tensor_tensor(prod_b[:], c0[:], 1.0, tpz[:], ALU.mult, ALU.mult, accum_out=bsum[:])
        nc.vector.scalar_tensor_tensor(negx[:, halves[0]], c0[:, halves[0]], mean[:], negk[:, halves[0]], ALU.subtract, ALU.mult)
        nc.vector.tensor_scalar(negb[:], mean[:], rho[:], bsum[:], ALU.mult, ALU.subtract)
        nc.vector.scalar_tensor_tensor(negx[:, halves[1]], c0[:, halves[1]], mean[:], negk[:, halves[1]], ALU.subtract, ALU.mult)
        for cols in halves:
            nc.vector.scalar_tensor_tensor(y[:, cols], gap[:, cols], negb[:], negx[:, cols], ALU.mult, ALU.subtract)
        nc.vector.tensor_tensor(placed[:].indirect(offsets[:]), y[:], part_sq[:], ALU.mult)

        first = 0
        for n, width in enumerate(STORE):
            cols = slice(first, first + width)
            result = tile("result%d" % n, [P, width], F32)
            nc.vector.scalar_tensor_tensor(result[:], placed[:, cols], rz, base_sb[:, cols], ALU.mult, ALU.add)
            nc.sync.dma_start(out=out[:, cols], in_=result[:])
            first = first + width
